import numpy as np
import ml_dtypes


def mxq(x, axis, fmt="e4m3"):
    dtype, down = {"e4m3": (ml_dtypes.float8_e4m3fn, 7), "e5m2": (ml_dtypes.float8_e5m2, 14)}[fmt]
    v = np.moveaxis(np.asarray(x, np.float32).astype(ml_dtypes.bfloat16).astype(np.float64), axis, -1)
    blocks = v.reshape(v.shape[:-1] + (-1, 32))
    amax = np.abs(blocks).max(-1, keepdims=True)
    byte = np.maximum(np.where(amax > 0, np.frexp(amax)[1] - 1 + 127, 0) - down, 1)
    scale = np.exp2(byte - 127.0)
    codes = (blocks / scale).astype(np.float32).astype(dtype).astype(np.float64)
    return np.moveaxis((codes * scale).reshape(v.shape), -1, axis)


WIDE = False


def mx_kscale(k):
    if not WIDE:
        return np.ones(k)
    levels = np.array([10, -10, 5, -5, 0])
    if k % 512:
        return np.exp2(np.random.permutation(np.resize(levels, k // 32))).repeat(32)
    a = np.empty((k // 512, 16))
    for p in range(k // 512):
        a[p, :8] = np.random.permutation(np.resize(levels, 8))
        for g in range(8):
            far = levels[np.abs(levels - a[p, g]) >= 10]
            a[p, g + 8] = far[np.random.randint(len(far))]
    return np.exp2(a.ravel()).repeat(32)


def f64(x):
    return np.asarray(x).astype(np.float64)


def striped(idx):
    return np.tile(idx.reshape(-1, 16).T, (8, 1)).astype(np.uint16)


def unstriped(offs):
    return offs[:16].T.reshape(-1).astype(np.int64)


def pack_weight(w):
    k, n = w.shape
    w = f64(np.asarray(w, np.float32).astype(ml_dtypes.bfloat16)).reshape(k // 32, 32, n)
    amax = np.abs(w).max(1)
    byte = np.clip(np.where(amax > 0, np.frexp(amax)[1] - 1 + 127 - 7, 1), 1, 254)
    scaled = (w * np.exp2(127.0 - byte)[:, None, :]).reshape(k, n).astype(np.float32)
    words = np.ascontiguousarray(scaled.reshape(k // 512, 128, 4, n).transpose(0, 1, 3, 2)).astype(ml_dtypes.float8_e4m3fn).view(np.uint8)
    return words, np.ascontiguousarray(byte.astype(np.uint8).reshape(k // 512, 16, n))


def unpack_weight(words, scales):
    g, p, n, _ = words.shape
    vals = np.ascontiguousarray(words).view(ml_dtypes.float8_e4m3fn).astype(np.float64) * np.repeat(np.exp2(scales.astype(np.float64) - 127.0), 8, axis=1)[..., None]
    return vals.transpose(0, 1, 3, 2).reshape(g * 512, n)


def sigmoid(v):
    return 1.0 / (1.0 + np.exp(-np.maximum(v, -700.0)))


K, T, S, N, H, U, W = 512, 2048, 512, 128, 512, 1024, 1024


def setup_inputs():
    n = np.random.standard_normal
    s = mx_kscale(K)[:, None]
    u = mx_kscale(H)
    packed_xT = pack_weight(n((K, T)) * s)
    packed_eT = pack_weight(n((K, W)) * s)
    return {
        "x_words": packed_xT[0],
        "x_scales": packed_xT[1],
        "w1": (n((K, H)) / np.sqrt(K) / s).astype(np.float32),
        "e_words": packed_eT[0],
        "e_scales": packed_eT[1],
        "w2": (n((K, H)) / np.sqrt(K) / s).astype(np.float32),
        "gn": (np.random.uniform(0.4, 1.6, (H, U))).astype(np.float32),
        "unit": (np.random.uniform(0.6, 1.4, (H, 1)) * u[:, None]).astype(np.float32),
        "w3": (n((H, N)) / np.sqrt(H) / u[:, None]).astype(np.float32),
        "feat": (n((N, U))).astype(np.float32),
        "offs": striped(np.random.permutation(T)[:S]),
        "lv2": striped(np.random.permutation(W)[:S]),
        "c1": striped(np.random.permutation(np.concatenate([np.arange(S), np.random.randint(0, S, U - S)]))),
        "c2": striped(np.random.permutation(np.concatenate([np.arange(S), np.random.randint(0, S, U - S)]))),
    }


def reference(x_words, x_scales, w1, e_words, e_scales, w2, gn, unit, w3, feat, offs, lv2, c1, c2):
    xq = unpack_weight(x_words, x_scales)[:, unstriped(offs)]
    y = mxq(f64(w1), 0, "e4m3").T @ xq
    s1 = y[:, unstriped(c1)]
    e_lv2 = unpack_weight(e_words, e_scales)[:, unstriped(lv2)]
    ye = mxq(f64(w2), 0, "e4m3").T @ e_lv2
    s2 = ye[:, unstriped(c2)]
    rec = s1 + f64(gn) * s2
    act = rec * sigmoid(rec)
    hid = f64(unit) * act
    rr = mxq(f64(w3), 0, "e4m3").T @ mxq(hid, 0, "e4m3")
    return rr + f64(feat)

@@ -1,0 +1,232 @@
+from contextlib import ExitStack
+
+import concourse.mybir as mybir
+
+K, T, S, N, H, U, W = 512, 2048, 512, 128, 512, 1024, 1024
+FLOPS = 2 * K * H * S * 2 + 2 * H * N * U
+
+F32 = mybir.dt.float32
+BF16 = mybir.dt.bfloat16
+I32 = mybir.dt.int32
+U32 = mybir.dt.uint32
+U16 = mybir.dt.uint16
+U8 = mybir.dt.uint8
+FP8X4 = mybir.dt.float8_e4m3fn_x4
+MULT = mybir.AluOpType.mult
+ADD = mybir.AluOpType.add
+SILU = mybir.ActivationFunctionType.Silu
+COPY = mybir.ActivationFunctionType.Copy
+
+P = 128
+PACK = 4
+PAD = 16
+HALF = U // 2
+CHUNKS = ((0, 512), (512, 256), (768, 128), (896, 128))
+
+
+def tile_picked_ysemid_gate_p_kernel(
+    tc, x_words, x_scales, w1, e_words, e_scales, w2, gn, unit, w3, feat, offs, lv2, c1, c2, out
+):
+    nc = tc.nc
+    with ExitStack() as ctx:
+        keep = ctx.enter_context(tc.tile_pool(name="keep", bufs=1))
+        ring = ctx.enter_context(tc.tile_pool(name="ring", bufs=2))
+        psum = ctx.enter_context(tc.psum_pool(name="psum", bufs=1))
+
+        def held(shape, dtype, name):
+            return keep.tile(shape, dtype, name=name, align_bytes=64)
+
+        offs_sb = held([P, S // 16], U16, "offs_sb")
+        lv2_sb = held([P, S // 16], U16, "lv2_sb")
+        c1_sb = held([P, U // 16], U16, "c1_sb")
+        c2_sb = held([P, U // 16], U16, "c2_sb")
+        e_table = held([P, W], I32, "e_table")
+        e_bytes = held([P, W], U8, "e_bytes")
+        x_table = held([P, T], I32, "x_table")
+        x_bytes = held([P, T], U8, "x_bytes")
+        w1_raw = [held([P, PACK, H // 2], F32, "w1_raw%d" % h) for h in range(2)]
+        w2_raw = [held([P, PACK, H // 2], F32, "w2_raw%d" % h) for h in range(2)]
+        w3_raw = held([P, PACK, N], F32, "w3_raw")
+        gn_sb = [[held([P, HALF], F32, "gn%d_%d" % (h, t)) for t in range(PACK)] for h in range(2)]
+        unit_sb = held([P, PACK], F32, "unit_sb")
+        feat_sb = held([P, U], F32, "feat_sb")
+        y_sb = [held([P, S + PAD], F32, "y%d" % t) for t in range(PACK)]
+        ye_sb = [held([P, S + PAD], F32, "ye%d" % t) for t in range(PACK)]
+
+        nc.vector.memset(e_bytes[:].bitcast(I32), 0)
+        nc.vector.memset(x_bytes[:].bitcast(I32), 0)
+        for t in range(PACK):
+            nc.vector.memset(ye_sb[t][:, S:], 0.0)
+        for t in range(PACK):
+            nc.vector.memset(y_sb[t][:, S:], 0.0)
+
+        def load_words(table, words):
+            nc.sync.dma_start(out=table[:], in_=words[0].rearrange("p n t -> p (n t)").bitcast(I32))
+
+        def load_bytes(plane, scales):
+            for q in range(4):
+                nc.sync.dma_start(
+                    out=plane[32 * q : 32 * q + 4, :].bitcast(I32),
+                    in_=scales[0, 4 * q : 4 * q + 4, :].bitcast(I32),
+                )
+
+        def load_weight_half(raw, w, h):
+            cols = slice(h * (H // 2), (h + 1) * (H // 2))
+            nc.sync.dma_start(out=raw[h][:], in_=w.rearrange("(p j) c -> p j c", j=PACK)[:, :, cols])
+
+        gn_rows = gn.rearrange("(p t) r -> p t r", t=PACK)
+
+        def load_gain(h, t):
+            nc.sync.dma_start(out=gn_sb[h][t][:], in_=gn_rows[:, t, h * HALF : (h + 1) * HALF])
+
+        load_words(e_table, e_words)
+        nc.sync.dma_start(lv2_sb[:], lv2)
+        load_bytes(e_bytes, e_scales)
+        load_weight_half(w2_raw, w2, 0)
+        load_weight_half(w2_raw, w2, 1)
+        nc.sync.dma_start(c2_sb[:], c2)
+        load_gain(0, 0)
+        load_gain(0, 1)
+        load_words(x_table, x_words)
+        nc.sync.dma_start(offs_sb[:], offs)
+        load_bytes(x_bytes, x_scales)
+        load_weight_half(w1_raw, w1, 0)
+        load_weight_half(w1_raw, w1, 1)
+        load_gain(0, 2)
+        load_gain(0, 3)
+        nc.sync.dma_start(c1_sb[:], c1)
+        load_gain(1, 0)
+        nc.sync.dma_start(out=unit_sb[:], in_=unit.rearrange("(p t) o -> p (t o)", t=PACK))
+        nc.sync.dma_start(out=w3_raw[:], in_=w3.rearrange("(p j) c -> p j c", j=PACK))
+        for t in range(1, PACK):
+            load_gain(1, t)
+        nc.sync.dma_start(out=feat_sb[:], in_=feat)
+
+        def pick(table, plane, offsets, name):
+            codes = held([P, S], U32, name + "_codes")
+            scales = held([P, S], U8, name + "_scales")
+            nc.vector.tensor_copy(codes[:], table[:].bitcast(U32).indirect(offsets[:]))
+            nc.vector.tensor_copy(scales[:], plane[:].indirect(offsets[:]))
+            return codes, scales
+
+        def deal(copy, grouped, raw, h):
+            m = H // PACK // 2
+            copy(
+                out=grouped[:].rearrange("p (t m j) -> p m t j", t=PACK, j=PACK)[:, h * m : (h + 1) * m, :, :],
+                in_=raw[h][:].rearrange("p j (m t) -> p m t j", t=PACK),
+            )
+
+        def project(w_codes, w_scales, codes, scales, dst, t):
+            acc = psum.tile([P, S], F32, name="acc", bufs=4)
+            cols = slice(t * P, (t + 1) * P)
+            nc.tensor.matmul_mx(
+                out=acc[:], lhsT=w_codes[:, cols].bitcast(FP8X4), lhsT_scale=w_scales[:, cols],
+                rhs=codes[:].bitcast(FP8X4), rhs_scale=scales[:], start=True, stop=True,
+            )
+            nc.scalar.copy(out=dst[:, :S], in_=acc[:])
+
+        w2_bf = held([P, PACK * H], BF16, "w2_bf")
+        w2_codes = held([P, H], U32, "w2_codes")
+        w2_scales = held([P, H], U8, "w2_scales")
+        e_codes, e_sc = pick(e_table, e_bytes, lv2_sb, "e")
+        deal(nc.scalar.copy, w2_bf, w2_raw, 0)
+        deal(nc.vector.tensor_copy, w2_bf, w2_raw, 1)
+        for t in range(PACK):
+            cols = slice(t * P, (t + 1) * P)
+            nc.vector.quantize_mx(
+                out=w2_codes[:, cols].bitcast(FP8X4), scales=w2_scales[:, cols],
+                in_=w2_bf[:, t * P * PACK : (t + 1) * P * PACK],
+            )
+            project(w2_codes, w2_scales, e_codes, e_sc, ye_sb[t], t)
+
+        gated = {}
+
+        def gate(c, t):
+            c0, n = CHUNKS[c]
+            h, lo = divmod(c0, HALF)
+            g = ring.tile([P, n], F32, name="gated", bufs=5, align_bytes=64)
+            nc.vector.tensor_tensor(
+                g[:], ye_sb[t][:].indirect(c2_sb[:, c0 // 16 : (c0 + n) // 16]), gn_sb[h][t][:, lo : lo + n], MULT
+            )
+            gated[(c, t)] = g
+
+        gate(0, 0)
+        gate(0, 1)
+
+        w1_bf = held([P, PACK * H], BF16, "w1_bf")
+        w1_codes = held([P, H], U32, "w1_codes")
+        w1_scales = held([P, H], U8, "w1_scales")
+        x_codes, x_sc = pick(x_table, x_bytes, offs_sb, "x")
+        deal(nc.scalar.copy, w1_bf, w1_raw, 0)
+        deal(nc.scalar.copy, w1_bf, w1_raw, 1)
+        gate(0, 2)
+        gate(0, 3)
+        nc.vector.quantize_mx(out=w1_codes[:].bitcast(FP8X4), scales=w1_scales[:], in_=w1_bf[:])
+        for t in range(PACK):
+            project(w1_codes, w1_scales, x_codes, x_sc, y_sb[t], t)
+        gate(1, 0)
+
+        w3_bf = held([P, PACK * N], BF16, "w3_bf")
+        w3_codes = held([P, N], U32, "w3_codes")
+        w3_scales = held([P, N], U8, "w3_scales")
+        nc.scalar.copy(
+            out=w3_bf[:].rearrange("p (c i j) -> p c j i", i=4, j=PACK),
+            in_=w3_raw[:].rearrange("p j (c i) -> p c j i", i=4),
+        )
+        nc.vector.quantize_mx(out=w3_codes[:].bitcast(FP8X4), scales=w3_scales[:], in_=w3_bf[:])
+
+        planes = {}
+
+        def hidden(c, t):
+            c0, n = CHUNKS[c]
+            rec = ring.tile([P, n], F32, name="rec", bufs=3, align_bytes=64)
+            nc.vector.tensor_tensor(
+                rec[:], y_sb[t][:].indirect(c1_sb[:, c0 // 16 : (c0 + n) // 16]), gated[(c, t)][:], ADD
+            )
+            act = ring.tile([P, n], F32, name="act", bufs=2, align_bytes=64)
+            nc.scalar.activation(act[:], rec[:], SILU)
+            if t == 0:
+                planes[c] = held([P, PACK, n], BF16, "planes%d" % c)
+            nc.scalar.activation(planes[c][:, t, :], act[:], COPY, scale=unit_sb[:, t : t + 1])
+
+        woven = {}
+
+        def weave(c, copy):
+            c0, n = CHUNKS[c]
+            woven[c] = held([P, n * PACK], BF16, "woven%d" % c)
+            copy(
+                out=woven[c][:].rearrange("p (c i t) -> p c t i", i=4, t=PACK),
+                in_=planes[c][:].rearrange("p t (c i) -> p c t i", i=4),
+            )
+
+        def finish(c):
+            c0, n = CHUNKS[c]
+            codes = held([P, n], U32, "hid_codes%d" % c)
+            scales = held([P, n], U8, "hid_scales%d" % c)
+            nc.vector.quantize_mx(out=codes[:].bitcast(FP8X4), scales=scales[:], in_=woven[c][:])
+            rr = psum.tile([P, n], F32, name="rr", bufs=2)
+            nc.tensor.matmul_mx(
+                out=rr[:], lhsT=w3_codes[:].bitcast(FP8X4), lhsT_scale=w3_scales[:],
+                rhs=codes[:].bitcast(FP8X4), rhs_scale=scales[:], start=True, stop=True,
+            )
+            return rr
+
+        def store(c, rr):
+            c0, n = CHUNKS[c]
+            res = held([P, n], F32, "res%d" % c)
+            nc.vector.tensor_tensor(res[:], rr[:], feat_sb[:, c0 : c0 + n], ADD)
+            nc.sync.dma_start(out=out[:, c0 : c0 + n], in_=res[:])
+
+        last = len(CHUNKS) - 1
+        for c in range(len(CHUNKS)):
+            for t in range(PACK):
+                if (c, t) not in gated:
+                    gate(c, t)
+            if c > 0:
+                rr = finish(c - 1)
+            for t in range(PACK):
+                hidden(c, t)
+                if c > 0 and t == 0:
+                    store(c - 1, rr)
+            weave(c, nc.vector.tensor_copy if c == last else nc.scalar.copy)
+        store(last, finish(last))

@@ -44,76 +44,75 @@ def tile_picked_ysemid_gate_p_kernel(
         e_bytes = held([P, W], U8, "e_bytes")
         x_table = held([P, T], I32, "x_table")
         x_bytes = held([P, T], U8, "x_bytes")
-        w1_raw = [held([P, PACK, H // 2], F32, "w1_raw%d" % h) for h in range(2)]
-        w2_raw = [held([P, PACK, H // 2], F32, "w2_raw%d" % h) for h in range(2)]
+        w1_raw = held([P, PACK, H], F32, "w1_raw")
+        w2_raw = held([P, PACK, H], F32, "w2_raw")
         w3_raw = held([P, PACK, N], F32, "w3_raw")
-        gn_sb = [[held([P, HALF], F32, "gn%d_%d" % (h, t)) for t in range(PACK)] for h in range(2)]
+        gn_sb = [[held([P, 2, HALF], F32, "gn%d_%d" % (h, u)) for u in range(2)] for h in range(2)]
         unit_sb = held([P, PACK], F32, "unit_sb")
         feat_sb = held([P, U], F32, "feat_sb")
         y_sb = [held([P, S + PAD], F32, "y%d" % t) for t in range(PACK)]
         ye_sb = [held([P, S + PAD], F32, "ye%d" % t) for t in range(PACK)]
 
         nc.vector.memset(e_bytes[:].bitcast(I32), 0)
-        nc.vector.memset(x_bytes[:].bitcast(I32), 0)
+        nc.gpsimd.memset(x_bytes[:].bitcast(I32), 0)
         for t in range(PACK):
-            nc.vector.memset(ye_sb[t][:, S:], 0.0)
+            nc.gpsimd.memset(ye_sb[t][:, S:], 0.0)
         for t in range(PACK):
-            nc.vector.memset(y_sb[t][:, S:], 0.0)
+            nc.gpsimd.memset(y_sb[t][:, S:], 0.0)
 
         def load_words(table, words):
             nc.sync.dma_start(out=table[:], in_=words[0].rearrange("p n t -> p (n t)").bitcast(I32))
 
-        def load_bytes(plane, scales):
+        def load_bytes(queue, plane, scales):
             for q in range(4):
-                nc.sync.dma_start(
+                queue.dma_start(
                     out=plane[32 * q : 32 * q + 4, :].bitcast(I32),
                     in_=scales[0, 4 * q : 4 * q + 4, :].bitcast(I32),
                 )
 
-        def load_weight_half(raw, w, h):
-            cols = slice(h * (H // 2), (h + 1) * (H // 2))
-            nc.sync.dma_start(out=raw[h][:], in_=w.rearrange("(p j) c -> p j c", j=PACK)[:, :, cols])
+        def load_weight(raw, w):
+            nc.sync.dma_start(out=raw[:], in_=w.rearrange("(p j) c -> p j c", j=PACK))
 
         gn_rows = gn.rearrange("(p t) r -> p t r", t=PACK)
 
-        def load_gain(h, t):
-            nc.sync.dma_start(out=gn_sb[h][t][:], in_=gn_rows[:, t, h * HALF : (h + 1) * HALF])
+        def load_gain(h, u):
+            nc.sync.dma_start(out=gn_sb[h][u][:], in_=gn_rows[:, 2 * u : 2 * u + 2, h * HALF : (h + 1) * HALF])
 
-        load_words(e_table, e_words)
         nc.sync.dma_start(lv2_sb[:], lv2)
-        load_bytes(e_bytes, e_scales)
-        load_weight_half(w2_raw, w2, 0)
-        load_weight_half(w2_raw, w2, 1)
         nc.sync.dma_start(c2_sb[:], c2)
+        load_words(e_table, e_words)
+        load_bytes(nc.sync, e_bytes, e_scales)
+        load_weight(w2_raw, w2)
         load_gain(0, 0)
-        load_gain(0, 1)
-        load_words(x_table, x_words)
         nc.sync.dma_start(offs_sb[:], offs)
-        load_bytes(x_bytes, x_scales)
-        load_weight_half(w1_raw, w1, 0)
-        load_weight_half(w1_raw, w1, 1)
-        load_gain(0, 2)
-        load_gain(0, 3)
+        load_bytes(nc.sync, x_bytes, x_scales)
+        load_words(x_table, x_words)
+        load_weight(w1_raw, w1)
+        load_gain(0, 1)
         nc.sync.dma_start(c1_sb[:], c1)
-        load_gain(1, 0)
         nc.sync.dma_start(out=unit_sb[:], in_=unit.rearrange("(p t) o -> p (t o)", t=PACK))
-        nc.sync.dma_start(out=w3_raw[:], in_=w3.rearrange("(p j) c -> p j c", j=PACK))
-        for t in range(1, PACK):
-            load_gain(1, t)
+        load_gain(1, 0)
+        load_gain(1, 1)
+        load_weight(w3_raw, w3)
         nc.sync.dma_start(out=feat_sb[:], in_=feat)
 
-        def pick(table, plane, offsets, name):
-            codes = held([P, S], U32, name + "_codes")
-            scales = held([P, S], U8, name + "_scales")
-            nc.vector.tensor_copy(codes[:], table[:].bitcast(U32).indirect(offsets[:]))
-            nc.vector.tensor_copy(scales[:], plane[:].indirect(offsets[:]))
-            return codes, scales
+        warm = held([P, 1], F32, "warm")
+        nc.scalar.activation(warm[:], ye_sb[0][:, S : S + 1], SILU)
 
-        def deal(copy, grouped, raw, h):
-            m = H // PACK // 2
+        def pick_words(table, offsets, name):
+            codes = held([P, S], U32, name)
+            nc.vector.tensor_copy(codes[:], table[:].bitcast(U32).indirect(offsets[:]))
+            return codes
+
+        def pick_bytes(plane, offsets, name):
+            scales = held([P, S], U8, name)
+            nc.vector.tensor_copy(scales[:], plane[:].indirect(offsets[:]))
+            return scales
+
+        def deal(copy, grouped, raw, ts):
             copy(
-                out=grouped[:].rearrange("p (t m j) -> p m t j", t=PACK, j=PACK)[:, h * m : (h + 1) * m, :, :],
-                in_=raw[h][:].rearrange("p j (m t) -> p m t j", t=PACK),
+                out=grouped[:].rearrange("p (t m j) -> p m t j", t=PACK, j=PACK)[:, :, ts, :],
+                in_=raw[:].rearrange("p j (m t) -> p m t j", t=PACK)[:, :, ts, :],
             )
 
         def project(w_codes, w_scales, codes, scales, dst, t):
@@ -128,9 +127,13 @@ def tile_picked_ysemid_gate_p_kernel(
         w2_bf = held([P, PACK * H], BF16, "w2_bf")
         w2_codes = held([P, H], U32, "w2_codes")
         w2_scales = held([P, H], U8, "w2_scales")
-        e_codes, e_sc = pick(e_table, e_bytes, lv2_sb, "e")
-        deal(nc.scalar.copy, w2_bf, w2_raw, 0)
-        deal(nc.vector.tensor_copy, w2_bf, w2_raw, 1)
+        w1_bf = held([P, PACK * H], BF16, "w1_bf")
+        w1_codes = held([P, H], U32, "w1_codes")
+        w1_scales = held([P, H], U8, "w1_scales")
+        e_codes = pick_words(e_table, lv2_sb, "e_codes")
+        e_sc = pick_bytes(e_bytes, lv2_sb, "e_sc")
+        deal(nc.vector.tensor_copy, w2_bf, w2_raw, slice(0, 2))
+        deal(nc.scalar.copy, w2_bf, w2_raw, slice(2, PACK))
         for t in range(PACK):
             cols = slice(t * P, (t + 1) * P)
             nc.vector.quantize_mx(
@@ -138,33 +141,32 @@ def tile_picked_ysemid_gate_p_kernel(
                 in_=w2_bf[:, t * P * PACK : (t + 1) * P * PACK],
             )
             project(w2_codes, w2_scales, e_codes, e_sc, ye_sb[t], t)
+        x_sc = pick_bytes(x_bytes, offs_sb, "x_sc")
 
         gated = {}
 
         def gate(c, t):
             c0, n = CHUNKS[c]
             h, lo = divmod(c0, HALF)
-            g = ring.tile([P, n], F32, name="gated", bufs=5, align_bytes=64)
+            g = ring.tile([P, n], F32, name="gated%d" % min(c, 1), bufs=2 if c else 4, align_bytes=64)
             nc.vector.tensor_tensor(
-                g[:], ye_sb[t][:].indirect(c2_sb[:, c0 // 16 : (c0 + n) // 16]), gn_sb[h][t][:, lo : lo + n], MULT
+                g[:], ye_sb[t][:].indirect(c2_sb[:, c0 // 16 : (c0 + n) // 16]), gn_sb[h][t // 2][:, t % 2, lo : lo + n], MULT
             )
             gated[(c, t)] = g
 
         gate(0, 0)
+        x_codes = pick_words(x_table, offs_sb, "x_codes")
         gate(0, 1)
-
-        w1_bf = held([P, PACK * H], BF16, "w1_bf")
-        w1_codes = held([P, H], U32, "w1_codes")
-        w1_scales = held([P, H], U8, "w1_scales")
-        x_codes, x_sc = pick(x_table, x_bytes, offs_sb, "x")
-        deal(nc.scalar.copy, w1_bf, w1_raw, 0)
-        deal(nc.scalar.copy, w1_bf, w1_raw, 1)
-        gate(0, 2)
-        gate(0, 3)
-        nc.vector.quantize_mx(out=w1_codes[:].bitcast(FP8X4), scales=w1_scales[:], in_=w1_bf[:])
-        for t in range(PACK):
-            project(w1_codes, w1_scales, x_codes, x_sc, y_sb[t], t)
-        gate(1, 0)
+        for u in range(2):
+            deal(nc.scalar.copy, w1_bf, w1_raw, slice(2 * u, 2 * u + 2))
+            cols = slice(2 * u * P, (2 * u + 2) * P)
+            nc.vector.quantize_mx(
+                out=w1_codes[:, cols].bitcast(FP8X4), scales=w1_scales[:, cols],
+                in_=w1_bf[:, 2 * u * P * PACK : (2 * u + 2) * P * PACK],
+            )
+            for t in range(2 * u, 2 * u + 2):
+                project(w1_codes, w1_scales, x_codes, x_sc, y_sb[t], t)
+            gate(0, 2 + u)
 
         w3_bf = held([P, PACK * N], BF16, "w3_bf")
         w3_codes = held([P, N], U32, "w3_codes")
@@ -176,6 +178,8 @@ def tile_picked_ysemid_gate_p_kernel(
         nc.vector.quantize_mx(out=w3_codes[:].bitcast(FP8X4), scales=w3_scales[:], in_=w3_bf[:])
 
         planes = {}
+        last = len(CHUNKS) - 1
+        last_act = held([P, PACK, CHUNKS[last][1]], F32, "last_act")
 
         def hidden(c, t):
             c0, n = CHUNKS[c]
@@ -183,6 +187,9 @@ def tile_picked_ysemid_gate_p_kernel(
             nc.vector.tensor_tensor(
                 rec[:], y_sb[t][:].indirect(c1_sb[:, c0 // 16 : (c0 + n) // 16]), gated[(c, t)][:], ADD
             )
+            if c == last:
+                nc.scalar.activation(last_act[:, t, :], rec[:], SILU)
+                return
             act = ring.tile([P, n], F32, name="act", bufs=2, align_bytes=64)
             nc.scalar.activation(act[:], rec[:], SILU)
             if t == 0:
@@ -191,10 +198,18 @@ def tile_picked_ysemid_gate_p_kernel(
 
         woven = {}
 
-        def weave(c, copy):
+        def weave(c):
             c0, n = CHUNKS[c]
             woven[c] = held([P, n * PACK], BF16, "woven%d" % c)
-            copy(
+            if c == last:
+                nc.vector.tensor_tensor(
+                    woven[c][:].rearrange("p (r t) -> p r t", t=PACK),
+                    last_act[:].rearrange("p t r -> p r t"),
+                    unit_sb[:].unsqueeze(1).to_broadcast([P, n, PACK]),
+                    MULT,
+                )
+                return
+            nc.scalar.copy(
                 out=woven[c][:].rearrange("p (c i t) -> p c t i", i=4, t=PACK),
                 in_=planes[c][:].rearrange("p t (c i) -> p c t i", i=4),
             )
@@ -217,16 +232,15 @@ def tile_picked_ysemid_gate_p_kernel(
             nc.vector.tensor_tensor(res[:], rr[:], feat_sb[:, c0 : c0 + n], ADD)
             nc.sync.dma_start(out=out[:, c0 : c0 + n], in_=res[:])
 
-        last = len(CHUNKS) - 1
-        for c in range(len(CHUNKS)):
-            for t in range(PACK):
-                if (c, t) not in gated:
-                    gate(c, t)
-            if c > 0:
+        steps = [(c, t) for c in range(len(CHUNKS)) for t in range(PACK)]
+        for i, (c, t) in enumerate(steps):
+            hidden(c, t)
+            if i + 2 < len(steps) and steps[i + 2] not in gated:
+                gate(*steps[i + 2])
+            if t == PACK - 1:
+                weave(c)
+            if c > 0 and t == 2:
                 rr = finish(c - 1)
-            for t in range(PACK):
-                hidden(c, t)
-                if c > 0 and t == 0:
-                    store(c - 1, rr)
-            weave(c, nc.vector.tensor_copy if c == last else nc.scalar.copy)
+            if c > 0 and t == 3:
+                store(c - 1, rr)
         store(last, finish(last))

@@ -3,7 +3,7 @@ from contextlib import ExitStack
 import concourse.mybir as mybir
 
 K, T, S, N, H, U, W = 512, 2048, 512, 128, 512, 1024, 1024
-FLOPS = 2 * K * H * S * 2 + 2 * H * N * U
+FLOPS = 2 * (2 * K * H * S) + 2 * H * N * U
 
 F32 = mybir.dt.float32
 BF16 = mybir.dt.bfloat16
@@ -19,9 +19,14 @@ COPY = mybir.ActivationFunctionType.Copy
 
 P = 128
 PACK = 4
-PAD = 16
+STRIPE = 16
+RUN = 4
+SPARE = 16
 HALF = U // 2
-CHUNKS = ((0, 512), (512, 256), (768, 128), (896, 128))
+CHUNKS = ((0, 512), (512, 256), (768, 256))
+VECTOR_SHARE = 88
+REC_BUFS = 5
+GATE_AHEAD = 2
 
 
 def tile_picked_ysemid_gate_p_kernel(
@@ -30,16 +35,16 @@ def tile_picked_ysemid_gate_p_kernel(
     nc = tc.nc
     with ExitStack() as ctx:
         keep = ctx.enter_context(tc.tile_pool(name="keep", bufs=1))
-        ring = ctx.enter_context(tc.tile_pool(name="ring", bufs=2))
+        ring = ctx.enter_context(tc.tile_pool(name="ring", bufs=REC_BUFS))
         psum = ctx.enter_context(tc.psum_pool(name="psum", bufs=1))
 
         def held(shape, dtype, name):
             return keep.tile(shape, dtype, name=name, align_bytes=64)
 
-        offs_sb = held([P, S // 16], U16, "offs_sb")
-        lv2_sb = held([P, S // 16], U16, "lv2_sb")
-        c1_sb = held([P, U // 16], U16, "c1_sb")
-        c2_sb = held([P, U // 16], U16, "c2_sb")
+        offs_sb = held([P, S // STRIPE], U16, "offs_sb")
+        lv2_sb = held([P, S // STRIPE], U16, "lv2_sb")
+        c1_sb = held([P, U // STRIPE], U16, "c1_sb")
+        c2_sb = held([P, U // STRIPE], U16, "c2_sb")
         e_table = held([P, W], I32, "e_table")
         e_bytes = held([P, W], U8, "e_bytes")
         x_table = held([P, T], I32, "x_table")
@@ -50,50 +55,47 @@ def tile_picked_ysemid_gate_p_kernel(
         gn_sb = [[held([P, 2, HALF], F32, "gn%d_%d" % (h, u)) for u in range(2)] for h in range(2)]
         unit_sb = held([P, PACK], F32, "unit_sb")
         feat_sb = held([P, U], F32, "feat_sb")
-        y_sb = [held([P, S + PAD], F32, "y%d" % t) for t in range(PACK)]
-        ye_sb = [held([P, S + PAD], F32, "ye%d" % t) for t in range(PACK)]
+        y_sb = [held([P, S + SPARE], F32, "y%d" % t) for t in range(PACK)]
+        ye_sb = [held([P, S + SPARE], F32, "ye%d" % t) for t in range(PACK)]
 
         nc.vector.memset(e_bytes[:].bitcast(I32), 0)
         nc.gpsimd.memset(x_bytes[:].bitcast(I32), 0)
-        for t in range(PACK):
-            nc.gpsimd.memset(ye_sb[t][:, S:], 0.0)
-        for t in range(PACK):
-            nc.gpsimd.memset(y_sb[t][:, S:], 0.0)
+        for plane in ye_sb + y_sb:
+            nc.gpsimd.memset(plane[:, S:], 0.0)
 
         def load_words(table, words):
             nc.sync.dma_start(out=table[:], in_=words[0].rearrange("p n t -> p (n t)").bitcast(I32))
 
-        def load_bytes(queue, plane, scales):
+        def load_bytes(table, scales):
             for q in range(4):
-                queue.dma_start(
-                    out=plane[32 * q : 32 * q + 4, :].bitcast(I32),
+                nc.sync.dma_start(
+                    out=table[32 * q : 32 * q + 4, :].bitcast(I32),
                     in_=scales[0, 4 * q : 4 * q + 4, :].bitcast(I32),
                 )
 
         def load_weight(raw, w):
             nc.sync.dma_start(out=raw[:], in_=w.rearrange("(p j) c -> p j c", j=PACK))
 
-        gn_rows = gn.rearrange("(p t) r -> p t r", t=PACK)
-
         def load_gain(h, u):
-            nc.sync.dma_start(out=gn_sb[h][u][:], in_=gn_rows[:, 2 * u : 2 * u + 2, h * HALF : (h + 1) * HALF])
+            rows = gn.rearrange("(p t) r -> p t r", t=PACK)
+            nc.sync.dma_start(out=gn_sb[h][u][:], in_=rows[:, 2 * u : 2 * u + 2, h * HALF : (h + 1) * HALF])
 
         nc.sync.dma_start(lv2_sb[:], lv2)
         nc.sync.dma_start(c2_sb[:], c2)
         load_words(e_table, e_words)
-        load_bytes(nc.sync, e_bytes, e_scales)
+        load_bytes(e_bytes, e_scales)
         load_weight(w2_raw, w2)
-        load_gain(0, 0)
         nc.sync.dma_start(offs_sb[:], offs)
-        load_bytes(nc.sync, x_bytes, x_scales)
-        load_words(x_table, x_words)
+        load_gain(0, 0)
+        load_bytes(x_bytes, x_scales)
         load_weight(w1_raw, w1)
+        load_words(x_table, x_words)
         load_gain(0, 1)
         nc.sync.dma_start(c1_sb[:], c1)
         nc.sync.dma_start(out=unit_sb[:], in_=unit.rearrange("(p t) o -> p (t o)", t=PACK))
         load_gain(1, 0)
-        load_gain(1, 1)
         load_weight(w3_raw, w3)
+        load_gain(1, 1)
         nc.sync.dma_start(out=feat_sb[:], in_=feat)
 
         warm = held([P, 1], F32, "warm")
@@ -104,121 +106,113 @@ def tile_picked_ysemid_gate_p_kernel(
             nc.vector.tensor_copy(codes[:], table[:].bitcast(U32).indirect(offsets[:]))
             return codes
 
-        def pick_bytes(plane, offsets, name):
+        def pick_bytes(table, offsets, name):
             scales = held([P, S], U8, name)
-            nc.vector.tensor_copy(scales[:], plane[:].indirect(offsets[:]))
+            nc.vector.tensor_copy(scales[:], table[:].indirect(offsets[:]))
             return scales
 
-        def deal(copy, grouped, raw, ts):
+        def deal(copy, grouped, raw, ms):
             copy(
-                out=grouped[:].rearrange("p (t m j) -> p m t j", t=PACK, j=PACK)[:, :, ts, :],
-                in_=raw[:].rearrange("p j (m t) -> p m t j", t=PACK)[:, :, ts, :],
+                out=grouped[:].rearrange("p (t m j) -> p m t j", t=PACK, j=PACK)[:, ms, :, :],
+                in_=raw[:].rearrange("p j (m t) -> p m t j", t=PACK)[:, ms, :, :],
             )
 
-        def project(w_codes, w_scales, codes, scales, dst, t):
-            acc = psum.tile([P, S], F32, name="acc", bufs=4)
+        def project(w_codes, w_scales, codes, scales, plane, t):
+            acc = psum.tile([P, S], F32, name="acc", bufs=PACK)
             cols = slice(t * P, (t + 1) * P)
             nc.tensor.matmul_mx(
                 out=acc[:], lhsT=w_codes[:, cols].bitcast(FP8X4), lhsT_scale=w_scales[:, cols],
                 rhs=codes[:].bitcast(FP8X4), rhs_scale=scales[:], start=True, stop=True,
             )
-            nc.scalar.copy(out=dst[:, :S], in_=acc[:])
+            nc.scalar.copy(out=plane[:, :S], in_=acc[:])
 
         w2_bf = held([P, PACK * H], BF16, "w2_bf")
         w2_codes = held([P, H], U32, "w2_codes")
         w2_scales = held([P, H], U8, "w2_scales")
-        w1_bf = held([P, PACK * H], BF16, "w1_bf")
-        w1_codes = held([P, H], U32, "w1_codes")
-        w1_scales = held([P, H], U8, "w1_scales")
         e_codes = pick_words(e_table, lv2_sb, "e_codes")
-        e_sc = pick_bytes(e_bytes, lv2_sb, "e_sc")
-        deal(nc.vector.tensor_copy, w2_bf, w2_raw, slice(0, 2))
-        deal(nc.scalar.copy, w2_bf, w2_raw, slice(2, PACK))
+        e_picked_scales = pick_bytes(e_bytes, lv2_sb, "e_picked_scales")
+        deal(nc.vector.tensor_copy, w2_bf, w2_raw, slice(0, VECTOR_SHARE))
+        deal(nc.scalar.copy, w2_bf, w2_raw, slice(VECTOR_SHARE, P))
         for t in range(PACK):
             cols = slice(t * P, (t + 1) * P)
             nc.vector.quantize_mx(
                 out=w2_codes[:, cols].bitcast(FP8X4), scales=w2_scales[:, cols],
                 in_=w2_bf[:, t * P * PACK : (t + 1) * P * PACK],
             )
-            project(w2_codes, w2_scales, e_codes, e_sc, ye_sb[t], t)
-        x_sc = pick_bytes(x_bytes, offs_sb, "x_sc")
+            project(w2_codes, w2_scales, e_codes, e_picked_scales, ye_sb[t], t)
+        x_picked_scales = pick_bytes(x_bytes, offs_sb, "x_picked_scales")
 
         gated = {}
 
         def gate(c, t):
-            c0, n = CHUNKS[c]
-            h, lo = divmod(c0, HALF)
-            g = ring.tile([P, n], F32, name="gated%d" % min(c, 1), bufs=2 if c else 4, align_bytes=64)
+            first, n = CHUNKS[c]
+            h, lo = divmod(first, HALF)
+            gated[(c, t)] = held([P, n], F32, "gated%d_%d" % (c, t))
             nc.vector.tensor_tensor(
-                g[:], ye_sb[t][:].indirect(c2_sb[:, c0 // 16 : (c0 + n) // 16]), gn_sb[h][t // 2][:, t % 2, lo : lo + n], MULT
+                gated[(c, t)][:],
+                ye_sb[t][:].indirect(c2_sb[:, first // STRIPE : (first + n) // STRIPE]),
+                gn_sb[h][t // 2][:, t % 2, lo : lo + n],
+                MULT,
             )
-            gated[(c, t)] = g
 
+        w1_bf = held([P, PACK * H], BF16, "w1_bf")
+        w1_codes = held([P, H], U32, "w1_codes")
+        w1_scales = held([P, H], U8, "w1_scales")
         gate(0, 0)
-        x_codes = pick_words(x_table, offs_sb, "x_codes")
         gate(0, 1)
-        for u in range(2):
-            deal(nc.scalar.copy, w1_bf, w1_raw, slice(2 * u, 2 * u + 2))
-            cols = slice(2 * u * P, (2 * u + 2) * P)
-            nc.vector.quantize_mx(
-                out=w1_codes[:, cols].bitcast(FP8X4), scales=w1_scales[:, cols],
-                in_=w1_bf[:, 2 * u * P * PACK : (2 * u + 2) * P * PACK],
-            )
-            for t in range(2 * u, 2 * u + 2):
-                project(w1_codes, w1_scales, x_codes, x_sc, y_sb[t], t)
-            gate(0, 2 + u)
+        x_codes = pick_words(x_table, offs_sb, "x_codes")
+        deal(nc.scalar.copy, w1_bf, w1_raw, slice(0, P))
+        nc.vector.quantize_mx(out=w1_codes[:].bitcast(FP8X4), scales=w1_scales[:], in_=w1_bf[:])
+        for t in range(PACK):
+            project(w1_codes, w1_scales, x_codes, x_picked_scales, y_sb[t], t)
+        gate(0, 2)
+        gate(0, 3)
 
         w3_bf = held([P, PACK * N], BF16, "w3_bf")
         w3_codes = held([P, N], U32, "w3_codes")
         w3_scales = held([P, N], U8, "w3_scales")
         nc.scalar.copy(
-            out=w3_bf[:].rearrange("p (c i j) -> p c j i", i=4, j=PACK),
-            in_=w3_raw[:].rearrange("p j (c i) -> p c j i", i=4),
+            out=w3_bf[:].rearrange("p (g r j) -> p g j r", r=RUN, j=PACK),
+            in_=w3_raw[:].rearrange("p j (g r) -> p g j r", r=RUN),
         )
         nc.vector.quantize_mx(out=w3_codes[:].bitcast(FP8X4), scales=w3_scales[:], in_=w3_bf[:])
 
-        planes = {}
         last = len(CHUNKS) - 1
+        hid_planes = [held([P, PACK, n], BF16, "hid_planes%d" % c) for c, (first, n) in enumerate(CHUNKS[:last])]
         last_act = held([P, PACK, CHUNKS[last][1]], F32, "last_act")
+        hid_bf = [held([P, n * PACK], BF16, "hid_bf%d" % c) for c, (first, n) in enumerate(CHUNKS)]
 
         def hidden(c, t):
-            c0, n = CHUNKS[c]
-            rec = ring.tile([P, n], F32, name="rec", bufs=3, align_bytes=64)
+            first, n = CHUNKS[c]
+            rec = ring.tile([P, n], F32, name="rec", align_bytes=64)
             nc.vector.tensor_tensor(
-                rec[:], y_sb[t][:].indirect(c1_sb[:, c0 // 16 : (c0 + n) // 16]), gated[(c, t)][:], ADD
+                rec[:], y_sb[t][:].indirect(c1_sb[:, first // STRIPE : (first + n) // STRIPE]), gated[(c, t)][:], ADD
             )
             if c == last:
                 nc.scalar.activation(last_act[:, t, :], rec[:], SILU)
-                return
-            act = ring.tile([P, n], F32, name="act", bufs=2, align_bytes=64)
-            nc.scalar.activation(act[:], rec[:], SILU)
-            if t == 0:
-                planes[c] = held([P, PACK, n], BF16, "planes%d" % c)
-            nc.scalar.activation(planes[c][:, t, :], act[:], COPY, scale=unit_sb[:, t : t + 1])
+            else:
+                act = held([P, n], F32, "act%d_%d" % (c, t))
+                nc.scalar.activation(act[:], rec[:], SILU)
+                nc.scalar.activation(hid_planes[c][:, t, :], act[:], COPY, scale=unit_sb[:, t : t + 1])
 
-        woven = {}
-
-        def weave(c):
-            c0, n = CHUNKS[c]
-            woven[c] = held([P, n * PACK], BF16, "woven%d" % c)
+        def interleave(c):
+            n = CHUNKS[c][1]
+            target = hid_bf[c][:].rearrange("p (g r t) -> p g t r", r=RUN, t=PACK)
             if c == last:
                 nc.vector.tensor_tensor(
-                    woven[c][:].rearrange("p (r t) -> p r t", t=PACK),
-                    last_act[:].rearrange("p t r -> p r t"),
-                    unit_sb[:].unsqueeze(1).to_broadcast([P, n, PACK]),
+                    target,
+                    last_act[:].rearrange("p t (g r) -> p g t r", r=RUN),
+                    unit_sb[:].unsqueeze(1).unsqueeze(3).to_broadcast([P, n // RUN, PACK, RUN]),
                     MULT,
                 )
-                return
-            nc.scalar.copy(
-                out=woven[c][:].rearrange("p (c i t) -> p c t i", i=4, t=PACK),
-                in_=planes[c][:].rearrange("p t (c i) -> p c t i", i=4),
-            )
+            else:
+                nc.scalar.copy(out=target, in_=hid_planes[c][:].rearrange("p t (g r) -> p g t r", r=RUN))
 
-        def finish(c):
-            c0, n = CHUNKS[c]
+        def last_product(c):
+            n = CHUNKS[c][1]
             codes = held([P, n], U32, "hid_codes%d" % c)
             scales = held([P, n], U8, "hid_scales%d" % c)
-            nc.vector.quantize_mx(out=codes[:].bitcast(FP8X4), scales=scales[:], in_=woven[c][:])
+            nc.vector.quantize_mx(out=codes[:].bitcast(FP8X4), scales=scales[:], in_=hid_bf[c][:])
             rr = psum.tile([P, n], F32, name="rr", bufs=2)
             nc.tensor.matmul_mx(
                 out=rr[:], lhsT=w3_codes[:].bitcast(FP8X4), lhsT_scale=w3_scales[:],
@@ -227,20 +221,20 @@ def tile_picked_ysemid_gate_p_kernel(
             return rr
 
         def store(c, rr):
-            c0, n = CHUNKS[c]
+            first, n = CHUNKS[c]
             res = held([P, n], F32, "res%d" % c)
-            nc.vector.tensor_tensor(res[:], rr[:], feat_sb[:, c0 : c0 + n], ADD)
-            nc.sync.dma_start(out=out[:, c0 : c0 + n], in_=res[:])
+            nc.vector.tensor_tensor(res[:], rr[:], feat_sb[:, first : first + n], ADD)
+            nc.sync.dma_start(out=out[:, first : first + n], in_=res[:])
 
         steps = [(c, t) for c in range(len(CHUNKS)) for t in range(PACK)]
         for i, (c, t) in enumerate(steps):
             hidden(c, t)
-            if i + 2 < len(steps) and steps[i + 2] not in gated:
-                gate(*steps[i + 2])
+            if i + GATE_AHEAD < len(steps) and steps[i + GATE_AHEAD] not in gated:
+                gate(*steps[i + GATE_AHEAD])
             if t == PACK - 1:
-                weave(c)
-            if c > 0 and t == 2:
-                rr = finish(c - 1)
-            if c > 0 and t == 3:
-                store(c - 1, rr)
-        store(last, finish(last))
+                interleave(c)
+            if c > 0 and t == PACK - 2:
+                rr_before = last_product(c - 1)
+            if c > 0 and t == PACK - 1:
+                store(c - 1, rr_before)
+        store(last, last_product(last))

@@ -24,9 +24,8 @@ RUN = 4
 SPARE = 16
 HALF = U // 2
 CHUNKS = ((0, 512), (512, 256), (768, 256))
+LAST = len(CHUNKS) - 1
 VECTOR_SHARE = 88
-REC_BUFS = 5
-GATE_AHEAD = 2
 
 
 def tile_picked_ysemid_gate_p_kernel(
@@ -35,7 +34,6 @@ def tile_picked_ysemid_gate_p_kernel(
     nc = tc.nc
     with ExitStack() as ctx:
         keep = ctx.enter_context(tc.tile_pool(name="keep", bufs=1))
-        ring = ctx.enter_context(tc.tile_pool(name="ring", bufs=REC_BUFS))
         psum = ctx.enter_context(tc.psum_pool(name="psum", bufs=1))
 
         def held(shape, dtype, name):
@@ -133,40 +131,41 @@ def tile_picked_ysemid_gate_p_kernel(
         e_picked_scales = pick_bytes(e_bytes, lv2_sb, "e_picked_scales")
         deal(nc.vector.tensor_copy, w2_bf, w2_raw, slice(0, VECTOR_SHARE))
         deal(nc.scalar.copy, w2_bf, w2_raw, slice(VECTOR_SHARE, P))
-        for t in range(PACK):
-            cols = slice(t * P, (t + 1) * P)
+        for u in range(2):
+            cols = slice(2 * u * P, (2 * u + 2) * P)
             nc.vector.quantize_mx(
                 out=w2_codes[:, cols].bitcast(FP8X4), scales=w2_scales[:, cols],
-                in_=w2_bf[:, t * P * PACK : (t + 1) * P * PACK],
+                in_=w2_bf[:, cols.start * PACK : cols.stop * PACK],
             )
-            project(w2_codes, w2_scales, e_codes, e_picked_scales, ye_sb[t], t)
+            for t in (2 * u, 2 * u + 1):
+                project(w2_codes, w2_scales, e_codes, e_picked_scales, ye_sb[t], t)
         x_picked_scales = pick_bytes(x_bytes, offs_sb, "x_picked_scales")
+
+        def entries(offsets, first, n):
+            return offsets[:, first // STRIPE : (first + n) // STRIPE]
 
         gated = {}
 
-        def gate(c, t):
-            first, n = CHUNKS[c]
-            h, lo = divmod(first, HALF)
-            gated[(c, t)] = held([P, n], F32, "gated%d_%d" % (c, t))
+        def gate(h, t, target):
             nc.vector.tensor_tensor(
-                gated[(c, t)][:],
-                ye_sb[t][:].indirect(c2_sb[:, first // STRIPE : (first + n) // STRIPE]),
-                gn_sb[h][t // 2][:, t % 2, lo : lo + n],
-                MULT,
+                target, ye_sb[t][:].indirect(entries(c2_sb, h * HALF, HALF)), gn_sb[h][t // 2][:, t % 2, :], MULT
             )
+            gated[(h, t)] = target
 
         w1_bf = held([P, PACK * H], BF16, "w1_bf")
         w1_codes = held([P, H], U32, "w1_codes")
         w1_scales = held([P, H], U8, "w1_scales")
-        gate(0, 0)
-        gate(0, 1)
+        early = [held([P, HALF], F32, "early%d" % i) for i in range(PACK + 1)]
+        gate(0, 0, early[0][:])
+        gate(0, 1, early[1][:])
         x_codes = pick_words(x_table, offs_sb, "x_codes")
         deal(nc.scalar.copy, w1_bf, w1_raw, slice(0, P))
         nc.vector.quantize_mx(out=w1_codes[:].bitcast(FP8X4), scales=w1_scales[:], in_=w1_bf[:])
         for t in range(PACK):
             project(w1_codes, w1_scales, x_codes, x_picked_scales, y_sb[t], t)
-        gate(0, 2)
-        gate(0, 3)
+        gate(0, 2, early[2][:])
+        gate(0, 3, early[3][:])
+        gate(1, 0, early[PACK][:])
 
         w3_bf = held([P, PACK * N], BF16, "w3_bf")
         w3_codes = held([P, N], U32, "w3_codes")
@@ -177,31 +176,28 @@ def tile_picked_ysemid_gate_p_kernel(
         )
         nc.vector.quantize_mx(out=w3_codes[:].bitcast(FP8X4), scales=w3_scales[:], in_=w3_bf[:])
 
-        last = len(CHUNKS) - 1
-        hid_planes = [held([P, PACK, n], BF16, "hid_planes%d" % c) for c, (first, n) in enumerate(CHUNKS[:last])]
-        last_act = held([P, PACK, CHUNKS[last][1]], F32, "last_act")
+        act = [held([P, PACK, HALF], F32, "act%d" % h) for h in range(2)]
+        hid_planes = [held([P, PACK, n], BF16, "hid_planes%d" % c) for c, (first, n) in enumerate(CHUNKS[:LAST])]
         hid_bf = [held([P, n * PACK], BF16, "hid_bf%d" % c) for c, (first, n) in enumerate(CHUNKS)]
 
-        def hidden(c, t):
-            first, n = CHUNKS[c]
-            rec = ring.tile([P, n], F32, name="rec", align_bytes=64)
+        def activate(t, first, n, rec):
+            h, lo = divmod(first, HALF)
             nc.vector.tensor_tensor(
-                rec[:], y_sb[t][:].indirect(c1_sb[:, first // STRIPE : (first + n) // STRIPE]), gated[(c, t)][:], ADD
+                rec, y_sb[t][:].indirect(entries(c1_sb, first, n)), gated[(h, t)][:, lo : lo + n], ADD
             )
-            if c == last:
-                nc.scalar.activation(last_act[:, t, :], rec[:], SILU)
-            else:
-                act = held([P, n], F32, "act%d_%d" % (c, t))
-                nc.scalar.activation(act[:], rec[:], SILU)
-                nc.scalar.activation(hid_planes[c][:, t, :], act[:], COPY, scale=unit_sb[:, t : t + 1])
+            nc.scalar.activation(act[h][:, t, lo : lo + n], rec, SILU)
+
+        def scale(c, t):
+            n = CHUNKS[c][1]
+            nc.scalar.activation(hid_planes[c][:, t, :], act[c][:, t, :n], COPY, scale=unit_sb[:, t : t + 1])
 
         def interleave(c):
-            n = CHUNKS[c][1]
+            first, n = CHUNKS[c]
             target = hid_bf[c][:].rearrange("p (g r t) -> p g t r", r=RUN, t=PACK)
-            if c == last:
+            if c == LAST:
                 nc.vector.tensor_tensor(
                     target,
-                    last_act[:].rearrange("p t (g r) -> p g t r", r=RUN),
+                    act[1][:, :, first - HALF :].rearrange("p t (g r) -> p g t r", r=RUN),
                     unit_sb[:].unsqueeze(1).unsqueeze(3).to_broadcast([P, n // RUN, PACK, RUN]),
                     MULT,
                 )
@@ -213,28 +209,39 @@ def tile_picked_ysemid_gate_p_kernel(
             codes = held([P, n], U32, "hid_codes%d" % c)
             scales = held([P, n], U8, "hid_scales%d" % c)
             nc.vector.quantize_mx(out=codes[:].bitcast(FP8X4), scales=scales[:], in_=hid_bf[c][:])
-            rr = psum.tile([P, n], F32, name="rr", bufs=2)
+            rr = psum.tile([P, n], F32, name="rr", bufs=len(CHUNKS))
             nc.tensor.matmul_mx(
                 out=rr[:], lhsT=w3_codes[:].bitcast(FP8X4), lhsT_scale=w3_scales[:],
                 rhs=codes[:].bitcast(FP8X4), rhs_scale=scales[:], start=True, stop=True,
             )
             return rr
 
-        def store(c, rr):
+        def store(c, rr, res):
             first, n = CHUNKS[c]
-            res = held([P, n], F32, "res%d" % c)
-            nc.vector.tensor_tensor(res[:], rr[:], feat_sb[:, first : first + n], ADD)
-            nc.sync.dma_start(out=out[:, first : first + n], in_=res[:])
+            nc.vector.tensor_tensor(res, rr[:], feat_sb[:, first : first + n], ADD)
+            nc.sync.dma_start(out=out[:, first : first + n], in_=res)
 
-        steps = [(c, t) for c in range(len(CHUNKS)) for t in range(PACK)]
-        for i, (c, t) in enumerate(steps):
-            hidden(c, t)
-            if i + GATE_AHEAD < len(steps) and steps[i + GATE_AHEAD] not in gated:
-                gate(*steps[i + GATE_AHEAD])
-            if t == PACK - 1:
-                interleave(c)
-            if c > 0 and t == PACK - 2:
-                rr_before = last_product(c - 1)
-            if c > 0 and t == PACK - 1:
-                store(c - 1, rr_before)
-        store(last, last_product(last))
+        recs = [held([P, HALF], F32, "rec%d" % i) for i in range(2 * PACK - 1)]
+        for t in range(PACK):
+            activate(t, 0, HALF, recs[t][:])
+            scale(0, t)
+        interleave(0)
+
+        for t in range(PACK - 1):
+            activate(t, HALF, HALF, recs[PACK + t][:])
+            scale(1, t)
+            gate(1, t + 1, act[0][:, t, :])
+        rr_first = last_product(0)
+        last_rec = hid_planes[0][:].rearrange("p t r -> p (t r)").bitcast(F32)
+        for c in (1, LAST):
+            first, n = CHUNKS[c]
+            activate(PACK - 1, first, n, last_rec[:, first - HALF : first - HALF + n])
+            if c < LAST:
+                scale(c, PACK - 1)
+        store(0, rr_first, held([P, CHUNKS[0][1]], F32, "res_first")[:])
+        interleave(1)
+        interleave(LAST)
+        rr_last = last_product(LAST)
+        rr_second = last_product(1)
+        store(LAST, rr_last, hid_bf[1][:].bitcast(F32)[:, : CHUNKS[LAST][1]])
+        store(1, rr_second, held([P, CHUNKS[1][1]], F32, "res_second")[:])

@@ -96,9 +96,6 @@ def tile_picked_ysemid_gate_p_kernel(
         load_gain(1, 1)
         nc.sync.dma_start(out=feat_sb[:], in_=feat)
 
-        warm = held([P, 1], F32, "warm")
-        nc.scalar.activation(warm[:], ye_sb[0][:, S : S + 1], SILU)
-
         def pick_words(table, offsets, name):
             codes = held([P, S], U32, name)
             nc.vector.tensor_copy(codes[:], table[:].bitcast(U32).indirect(offsets[:]))

from contextlib import ExitStack

import concourse.mybir as mybir

K, T, S, N, H, U, W = 512, 2048, 512, 128, 512, 1024, 1024
FLOPS = 2 * (2 * K * H * S) + 2 * H * N * U

F32 = mybir.dt.float32
BF16 = mybir.dt.bfloat16
I32 = mybir.dt.int32
U32 = mybir.dt.uint32
U16 = mybir.dt.uint16
U8 = mybir.dt.uint8
FP8X4 = mybir.dt.float8_e4m3fn_x4
MULT = mybir.AluOpType.mult
ADD = mybir.AluOpType.add
SILU = mybir.ActivationFunctionType.Silu
COPY = mybir.ActivationFunctionType.Copy

P = 128
PACK = 4
STRIPE = 16
RUN = 4
SPARE = 16
HALF = U // 2
CHUNKS = ((0, 512), (512, 256), (768, 256))
LAST = len(CHUNKS) - 1
VECTOR_SHARE = 88


def tile_picked_ysemid_gate_p_kernel(
    tc, x_words, x_scales, w1, e_words, e_scales, w2, gn, unit, w3, feat, offs, lv2, c1, c2, out
):
    nc = tc.nc
    with ExitStack() as ctx:
        keep = ctx.enter_context(tc.tile_pool(name="keep", bufs=1))
        psum = ctx.enter_context(tc.psum_pool(name="psum", bufs=1))

        def held(shape, dtype, name):
            return keep.tile(shape, dtype, name=name, align_bytes=64)

        offs_sb = held([P, S // STRIPE], U16, "offs_sb")
        lv2_sb = held([P, S // STRIPE], U16, "lv2_sb")
        c1_sb = held([P, U // STRIPE], U16, "c1_sb")
        c2_sb = held([P, U // STRIPE], U16, "c2_sb")
        e_table = held([P, W], I32, "e_table")
        e_bytes = held([P, W], U8, "e_bytes")
        x_table = held([P, T], I32, "x_table")
        x_bytes = held([P, T], U8, "x_bytes")
        w1_raw = held([P, PACK, H], F32, "w1_raw")
        w2_raw = held([P, PACK, H], F32, "w2_raw")
        w3_raw = held([P, PACK, N], F32, "w3_raw")
        gn_sb = [[held([P, 2, HALF], F32, "gn%d_%d" % (h, u)) for u in range(2)] for h in range(2)]
        unit_sb = held([P, PACK], F32, "unit_sb")
        feat_sb = held([P, U], F32, "feat_sb")
        y_sb = [held([P, S + SPARE], F32, "y%d" % t) for t in range(PACK)]
        ye_sb = [held([P, S + SPARE], F32, "ye%d" % t) for t in range(PACK)]

        nc.vector.memset(e_bytes[:].bitcast(I32), 0)
        nc.gpsimd.memset(x_bytes[:].bitcast(I32), 0)
        for plane in ye_sb + y_sb:
            nc.gpsimd.memset(plane[:, S:], 0.0)

        def load_words(table, words):
            nc.sync.dma_start(out=table[:], in_=words[0].rearrange("p n t -> p (n t)").bitcast(I32))

        def load_bytes(table, scales):
            for q in range(4):
                nc.sync.dma_start(
                    out=table[32 * q : 32 * q + 4, :].bitcast(I32),
                    in_=scales[0, 4 * q : 4 * q + 4, :].bitcast(I32),
                )

        def load_weight(raw, w):
            nc.sync.dma_start(out=raw[:], in_=w.rearrange("(p j) c -> p j c", j=PACK))

        def load_gain(h, u):
            rows = gn.rearrange("(p t) r -> p t r", t=PACK)
            nc.sync.dma_start(out=gn_sb[h][u][:], in_=rows[:, 2 * u : 2 * u + 2, h * HALF : (h + 1) * HALF])

        nc.sync.dma_start(lv2_sb[:], lv2)
        nc.sync.dma_start(c2_sb[:], c2)
        load_words(e_table, e_words)
        load_bytes(e_bytes, e_scales)
        load_weight(w2_raw, w2)
        nc.sync.dma_start(offs_sb[:], offs)
        load_gain(0, 0)
        load_bytes(x_bytes, x_scales)
        load_weight(w1_raw, w1)
        load_words(x_table, x_words)
        load_gain(0, 1)
        nc.sync.dma_start(c1_sb[:], c1)
        nc.sync.dma_start(out=unit_sb[:], in_=unit.rearrange("(p t) o -> p (t o)", t=PACK))
        load_gain(1, 0)
        load_weight(w3_raw, w3)
        load_gain(1, 1)
        nc.sync.dma_start(out=feat_sb[:], in_=feat)

        def pick_words(table, offsets, name):
            codes = held([P, S], U32, name)
            nc.vector.tensor_copy(codes[:], table[:].bitcast(U32).indirect(offsets[:]))
            return codes

        def pick_bytes(table, offsets, name):
            scales = held([P, S], U8, name)
            nc.vector.tensor_copy(scales[:], table[:].indirect(offsets[:]))
            return scales

        def deal(copy, grouped, raw, ms):
            copy(
                out=grouped[:].rearrange("p (t m j) -> p m t j", t=PACK, j=PACK)[:, ms, :, :],
                in_=raw[:].rearrange("p j (m t) -> p m t j", t=PACK)[:, ms, :, :],
            )

        def project(w_codes, w_scales, codes, scales, plane, t):
            acc = psum.tile([P, S], F32, name="acc", bufs=PACK)
            cols = slice(t * P, (t + 1) * P)
            nc.tensor.matmul_mx(
                out=acc[:], lhsT=w_codes[:, cols].bitcast(FP8X4), lhsT_scale=w_scales[:, cols],
                rhs=codes[:].bitcast(FP8X4), rhs_scale=scales[:], start=True, stop=True,
            )
            nc.scalar.copy(out=plane[:, :S], in_=acc[:])

        w2_bf = held([P, PACK * H], BF16, "w2_bf")
        w2_codes = held([P, H], U32, "w2_codes")
        w2_scales = held([P, H], U8, "w2_scales")
        e_codes = pick_words(e_table, lv2_sb, "e_codes")
        e_picked_scales = pick_bytes(e_bytes, lv2_sb, "e_picked_scales")
        deal(nc.vector.tensor_copy, w2_bf, w2_raw, slice(0, VECTOR_SHARE))
        deal(nc.scalar.copy, w2_bf, w2_raw, slice(VECTOR_SHARE, P))
        for u in range(2):
            cols = slice(2 * u * P, (2 * u + 2) * P)
            nc.vector.quantize_mx(
                out=w2_codes[:, cols].bitcast(FP8X4), scales=w2_scales[:, cols],
                in_=w2_bf[:, cols.start * PACK : cols.stop * PACK],
            )
            for t in (2 * u, 2 * u + 1):
                project(w2_codes, w2_scales, e_codes, e_picked_scales, ye_sb[t], t)
        x_picked_scales = pick_bytes(x_bytes, offs_sb, "x_picked_scales")

        def entries(offsets, first, n):
            return offsets[:, first // STRIPE : (first + n) // STRIPE]

        gated = {}

        def gate(h, t, target):
            nc.vector.tensor_tensor(
                target, ye_sb[t][:].indirect(entries(c2_sb, h * HALF, HALF)), gn_sb[h][t // 2][:, t % 2, :], MULT
            )
            gated[(h, t)] = target

        w1_bf = held([P, PACK * H], BF16, "w1_bf")
        w1_codes = held([P, H], U32, "w1_codes")
        w1_scales = held([P, H], U8, "w1_scales")
        early = [held([P, HALF], F32, "early%d" % i) for i in range(PACK + 1)]
        gate(0, 0, early[0][:])
        gate(0, 1, early[1][:])
        x_codes = pick_words(x_table, offs_sb, "x_codes")
        deal(nc.scalar.copy, w1_bf, w1_raw, slice(0, P))
        nc.vector.quantize_mx(out=w1_codes[:].bitcast(FP8X4), scales=w1_scales[:], in_=w1_bf[:])
        for t in range(PACK):
            project(w1_codes, w1_scales, x_codes, x_picked_scales, y_sb[t], t)
        gate(0, 2, early[2][:])
        gate(0, 3, early[3][:])
        gate(1, 0, early[PACK][:])

        w3_bf = held([P, PACK * N], BF16, "w3_bf")
        w3_codes = held([P, N], U32, "w3_codes")
        w3_scales = held([P, N], U8, "w3_scales")
        nc.scalar.copy(
            out=w3_bf[:].rearrange("p (g r j) -> p g j r", r=RUN, j=PACK),
            in_=w3_raw[:].rearrange("p j (g r) -> p g j r", r=RUN),
        )
        nc.vector.quantize_mx(out=w3_codes[:].bitcast(FP8X4), scales=w3_scales[:], in_=w3_bf[:])

        act = [held([P, PACK, HALF], F32, "act%d" % h) for h in range(2)]
        hid_planes = [held([P, PACK, n], BF16, "hid_planes%d" % c) for c, (first, n) in enumerate(CHUNKS[:LAST])]
        hid_bf = [held([P, n * PACK], BF16, "hid_bf%d" % c) for c, (first, n) in enumerate(CHUNKS)]

        def activate(t, first, n, rec):
            h, lo = divmod(first, HALF)
            nc.vector.tensor_tensor(
                rec, y_sb[t][:].indirect(entries(c1_sb, first, n)), gated[(h, t)][:, lo : lo + n], ADD
            )
            nc.scalar.activation(act[h][:, t, lo : lo + n], rec, SILU)

        def scale(c, t):
            n = CHUNKS[c][1]
            nc.scalar.activation(hid_planes[c][:, t, :], act[c][:, t, :n], COPY, scale=unit_sb[:, t : t + 1])

        def interleave(c):
            first, n = CHUNKS[c]
            target = hid_bf[c][:].rearrange("p (g r t) -> p g t r", r=RUN, t=PACK)
            if c == LAST:
                nc.vector.tensor_tensor(
                    target,
                    act[1][:, :, first - HALF :].rearrange("p t (g r) -> p g t r", r=RUN),
                    unit_sb[:].unsqueeze(1).unsqueeze(3).to_broadcast([P, n // RUN, PACK, RUN]),
                    MULT,
                )
            else:
                nc.scalar.copy(out=target, in_=hid_planes[c][:].rearrange("p t (g r) -> p g t r", r=RUN))

        def last_product(c):
            n = CHUNKS[c][1]
            codes = held([P, n], U32, "hid_codes%d" % c)
            scales = held([P, n], U8, "hid_scales%d" % c)
            nc.vector.quantize_mx(out=codes[:].bitcast(FP8X4), scales=scales[:], in_=hid_bf[c][:])
            rr = psum.tile([P, n], F32, name="rr", bufs=len(CHUNKS))
            nc.tensor.matmul_mx(
                out=rr[:], lhsT=w3_codes[:].bitcast(FP8X4), lhsT_scale=w3_scales[:],
                rhs=codes[:].bitcast(FP8X4), rhs_scale=scales[:], start=True, stop=True,
            )
            return rr

        def store(c, rr, res):
            first, n = CHUNKS[c]
            nc.vector.tensor_tensor(res, rr[:], feat_sb[:, first : first + n], ADD)
            nc.sync.dma_start(out=out[:, first : first + n], in_=res)

        recs = [held([P, HALF], F32, "rec%d" % i) for i in range(2 * PACK - 1)]
        for t in range(PACK):
            activate(t, 0, HALF, recs[t][:])
            scale(0, t)
        interleave(0)

        for t in range(PACK - 1):
            activate(t, HALF, HALF, recs[PACK + t][:])
            scale(1, t)
            gate(1, t + 1, act[0][:, t, :])
        rr_first = last_product(0)
        last_rec = hid_planes[0][:].rearrange("p t r -> p (t r)").bitcast(F32)
        for c in (1, LAST):
            first, n = CHUNKS[c]
            activate(PACK - 1, first, n, last_rec[:, first - HALF : first - HALF + n])
            if c < LAST:
                scale(c, PACK - 1)
        store(0, rr_first, held([P, CHUNKS[0][1]], F32, "res_first")[:])
        interleave(1)
        interleave(LAST)
        rr_last = last_product(LAST)
        rr_second = last_product(1)
        store(LAST, rr_last, hid_bf[1][:].bitcast(F32)[:, : CHUNKS[LAST][1]])
        store(1, rr_second, held([P, CHUNKS[1][1]], F32, "res_second")[:])
